import numpy as np
import ml_dtypes

BF16 = ml_dtypes.bfloat16


def bf(x):
    return np.asarray(x, np.float32).astype(BF16)


def f32(x):
    return np.asarray(x, np.float32)


def f64(x):
    return np.asarray(x).astype(np.float64)


def striped(idx):
    return np.tile(idx.reshape(-1, 16).T, (8, 1))


S, K, M, N, D, V = 512, 512, 128, 1024, 8, 128


def setup_inputs():
    return {"table": bf(np.random.standard_normal((K, S))), "w": bf(np.random.standard_normal((K, M)) / np.sqrt(K)), "b": f32(0.5 * np.random.standard_normal((M, 1))), "offs": striped(np.random.permutation(np.tile(np.arange(S), 2))[:N])}


def reference(table, w, b, offs):
    idx = offs[:16].T.reshape(-1)
    x = f64(table)[:, idx]
    y = f64(w).T @ x
    z = np.tanh(y + f64(b))
    return z.reshape(M, V, D).max(axis=2)

@@ -1,0 +1,56 @@
+import concourse.mybir as mybir
+
+BF16, F32, U16 = mybir.dt.bfloat16, mybir.dt.float32, mybir.dt.uint16
+TANH = mybir.ActivationFunctionType.Tanh
+MAX = mybir.AluOpType.max
+X = mybir.AxisListType.X
+
+P = 128
+K, S, M, N = 512, 512, 128, 1024
+NEIGHBOURS = 8
+PIECE = 256
+K_BLOCKS = K // P
+PIECES = N // PIECE
+PIECE_COLS = PIECE // 16
+PIECE_NODES = PIECE // NEIGHBOURS
+
+FLOPS = 2 * K * M * N
+
+
+def tile_gather_matmul_kernel(tc, table, w, b, offs, out):
+    nc = tc.nc
+    with (
+        tc.tile_pool(name="held", bufs=1) as held,
+        tc.tile_pool(name="work", bufs=2) as work,
+        tc.psum_pool(name="psum", bufs=1) as psum,
+    ):
+        offsets = held.tile([P, N // 16], U16, name="offsets")
+        nc.sync.dma_start(offsets[:], offs)
+        weights = held.tile([P, K_BLOCKS, M], BF16, name="weights")
+        nc.scalar.dma_start(weights[:], w.rearrange("(a p) m -> p a m", p=P))
+        windows = [held.tile([P, S], BF16, name=f"window{a}") for a in range(K_BLOCKS)]
+        for a in range(K_BLOCKS):
+            queue = nc.sync if a % 2 == 0 else nc.scalar
+            queue.dma_start(windows[a][:], table[a * P : (a + 1) * P, :])
+        bias = held.tile([P, 1], F32, name="bias")
+        nc.gpsimd.dma_start(bias[:], b)
+
+        banks = [psum.tile([P, PIECE], F32, name=f"bank{q}") for q in range(PIECES)]
+        for a in range(K_BLOCKS):
+            for q in range(PIECES):
+                picked = windows[a][:].indirect(offsets[:, q * PIECE_COLS : (q + 1) * PIECE_COLS])
+                nc.tensor.matmul(
+                    banks[q][:], weights[:, a, :], picked,
+                    start=(a == 0), stop=(a == K_BLOCKS - 1),
+                )
+
+        pooled = held.tile([P, N // NEIGHBOURS], F32, name="pooled")
+        for q in range(PIECES):
+            z = work.tile([P, PIECE], F32, name="z")
+            nc.scalar.activation(z[:], banks[q][:], TANH, bias=bias[:, 0:1])
+            nc.vector.tensor_reduce(
+                pooled[:, q * PIECE_NODES : (q + 1) * PIECE_NODES],
+                z[:].rearrange("p (v t) -> p v t", t=NEIGHBOURS),
+                axis=X, op=MAX,
+            )
+        nc.sync.dma_start(out, pooled[:])

@@ -21,19 +21,17 @@ def tile_gather_matmul_kernel(tc, table, w, b, offs, out):
     nc = tc.nc
     with (
         tc.tile_pool(name="held", bufs=1) as held,
-        tc.tile_pool(name="work", bufs=2) as work,
         tc.psum_pool(name="psum", bufs=1) as psum,
     ):
         offsets = held.tile([P, N // 16], U16, name="offsets")
         nc.sync.dma_start(offsets[:], offs)
         weights = held.tile([P, K_BLOCKS, M], BF16, name="weights")
-        nc.scalar.dma_start(weights[:], w.rearrange("(a p) m -> p a m", p=P))
+        nc.sync.dma_start(weights[:], w.rearrange("(a p) m -> p a m", p=P))
         windows = [held.tile([P, S], BF16, name=f"window{a}") for a in range(K_BLOCKS)]
         for a in range(K_BLOCKS):
-            queue = nc.sync if a % 2 == 0 else nc.scalar
-            queue.dma_start(windows[a][:], table[a * P : (a + 1) * P, :])
+            nc.scalar.dma_start(windows[a][:], table[a * P : (a + 1) * P, :])
         bias = held.tile([P, 1], F32, name="bias")
-        nc.gpsimd.dma_start(bias[:], b)
+        nc.sync.dma_start(bias[:], b)
 
         banks = [psum.tile([P, PIECE], F32, name=f"bank{q}") for q in range(PIECES)]
         for a in range(K_BLOCKS):
@@ -45,12 +43,13 @@ def tile_gather_matmul_kernel(tc, table, w, b, offs, out):
                 )
 
         pooled = held.tile([P, N // NEIGHBOURS], F32, name="pooled")
+        result = held.tile([P, N // NEIGHBOURS], F32, name="result")
         for q in range(PIECES):
-            z = work.tile([P, PIECE], F32, name="z")
-            nc.scalar.activation(z[:], banks[q][:], TANH, bias=bias[:, 0:1])
+            nodes = slice(q * PIECE_NODES, (q + 1) * PIECE_NODES)
             nc.vector.tensor_reduce(
-                pooled[:, q * PIECE_NODES : (q + 1) * PIECE_NODES],
-                z[:].rearrange("p (v t) -> p v t", t=NEIGHBOURS),
+                pooled[:, nodes],
+                banks[q][:].rearrange("p (v t) -> p v t", t=NEIGHBOURS),
                 axis=X, op=MAX,
             )
-        nc.sync.dma_start(out, pooled[:])
+            nc.scalar.activation(result[:, nodes], pooled[:, nodes], TANH, bias=bias[:, 0:1])
+        nc.sync.dma_start(out, result[:])

@@ -13,6 +13,8 @@ K_BLOCKS = K // P
 PIECES = N // PIECE
 PIECE_COLS = PIECE // 16
 PIECE_NODES = PIECE // NEIGHBOURS
+IDLE_REPEATS = 4
+IDLE_MATMULS = 5
 
 FLOPS = 2 * K * M * N
 
@@ -32,6 +34,15 @@ def tile_gather_matmul_kernel(tc, table, w, b, offs, out):
             nc.scalar.dma_start(windows[a][:], table[a * P : (a + 1) * P, :])
         bias = held.tile([P, 1], F32, name="bias")
         nc.sync.dma_start(bias[:], b)
+
+        zeros = held.tile([P, P], BF16, name="zeros")
+        nc.gpsimd.memset(zeros[:], 0.0)
+        idle_bank = psum.tile([P, IDLE_REPEATS, P], F32, name="idle_bank")
+        for i in range(IDLE_MATMULS):
+            nc.tensor.matmul(
+                idle_bank[:], zeros[:], zeros[:].unsqueeze(1).to_broadcast([P, IDLE_REPEATS, P]),
+                start=True, stop=True,
+            )
 
         banks = [psum.tile([P, PIECE], F32, name=f"bank{q}") for q in range(PIECES)]
         for a in range(K_BLOCKS):

@@ -13,8 +13,6 @@ K_BLOCKS = K // P
 PIECES = N // PIECE
 PIECE_COLS = PIECE // 16
 PIECE_NODES = PIECE // NEIGHBOURS
-IDLE_REPEATS = 4
-IDLE_MATMULS = 5
 
 FLOPS = 2 * K * M * N
 
@@ -28,21 +26,13 @@ def tile_gather_matmul_kernel(tc, table, w, b, offs, out):
         offsets = held.tile([P, N // 16], U16, name="offsets")
         nc.sync.dma_start(offsets[:], offs)
         weights = held.tile([P, K_BLOCKS, M], BF16, name="weights")
-        nc.sync.dma_start(weights[:], w.rearrange("(a p) m -> p a m", p=P))
+        nc.sync.dma_start(weights[:], w.rearrange("(p a) m -> p a m", a=K_BLOCKS))
+        table_blocks = table.rearrange("(p a) s -> a p s", a=K_BLOCKS)
         windows = [held.tile([P, S], BF16, name=f"window{a}") for a in range(K_BLOCKS)]
         for a in range(K_BLOCKS):
-            nc.scalar.dma_start(windows[a][:], table[a * P : (a + 1) * P, :])
+            nc.scalar.dma_start(windows[a][:], table_blocks[a])
         bias = held.tile([P, 1], F32, name="bias")
         nc.sync.dma_start(bias[:], b)
-
-        zeros = held.tile([P, P], BF16, name="zeros")
-        nc.gpsimd.memset(zeros[:], 0.0)
-        idle_bank = psum.tile([P, IDLE_REPEATS, P], F32, name="idle_bank")
-        for i in range(IDLE_MATMULS):
-            nc.tensor.matmul(
-                idle_bank[:], zeros[:], zeros[:].unsqueeze(1).to_broadcast([P, IDLE_REPEATS, P]),
-                start=True, stop=True,
-            )
 
         banks = [psum.tile([P, PIECE], F32, name=f"bank{q}") for q in range(PIECES)]
         for a in range(K_BLOCKS):

@@ -35,17 +35,23 @@ def tile_gather_matmul_kernel(tc, table, w, b, offs, out):
         nc.sync.dma_start(bias[:], b)
 
         banks = [psum.tile([P, PIECE], F32, name=f"bank{q}") for q in range(PIECES)]
-        for a in range(K_BLOCKS):
+
+        def gathered_matmul(a, q):
+            picked = windows[a][:].indirect(offsets[:, q * PIECE_COLS : (q + 1) * PIECE_COLS])
+            nc.tensor.matmul(
+                banks[q][:], weights[:, a, :], picked,
+                start=(a == 0), stop=(a == K_BLOCKS - 1),
+            )
+
+        for a in range(K_BLOCKS // 2):
             for q in range(PIECES):
-                picked = windows[a][:].indirect(offsets[:, q * PIECE_COLS : (q + 1) * PIECE_COLS])
-                nc.tensor.matmul(
-                    banks[q][:], weights[:, a, :], picked,
-                    start=(a == 0), stop=(a == K_BLOCKS - 1),
-                )
+                gathered_matmul(a, q)
 
         pooled = held.tile([P, N // NEIGHBOURS], F32, name="pooled")
         result = held.tile([P, N // NEIGHBOURS], F32, name="result")
         for q in range(PIECES):
+            for a in range(K_BLOCKS // 2, K_BLOCKS):
+                gathered_matmul(a, q)
             nodes = slice(q * PIECE_NODES, (q + 1) * PIECE_NODES)
             nc.vector.tensor_reduce(
                 pooled[:, nodes],

@@ -8,11 +8,9 @@ X = mybir.AxisListType.X
 P = 128
 K, S, M, N = 512, 512, 128, 1024
 NEIGHBOURS = 8
-PIECE = 256
 K_BLOCKS = K // P
-PIECES = N // PIECE
-PIECE_COLS = PIECE // 16
-PIECE_NODES = PIECE // NEIGHBOURS
+PIECE = 256
+BANK_ENTRIES = (2 * PIECE, PIECE, PIECE)
 
 FLOPS = 2 * K * M * N
 
@@ -34,28 +32,38 @@ def tile_gather_matmul_kernel(tc, table, w, b, offs, out):
         bias = held.tile([P, 1], F32, name="bias")
         nc.sync.dma_start(bias[:], b)
 
-        banks = [psum.tile([P, PIECE], F32, name=f"bank{q}") for q in range(PIECES)]
+        banks = [
+            psum.tile([P, entries], F32, name=f"bank{i}") for i, entries in enumerate(BANK_ENTRIES)
+        ]
+        first_entry = [sum(BANK_ENTRIES[:i]) for i in range(len(BANK_ENTRIES))]
 
-        def gathered_matmul(a, q):
-            picked = windows[a][:].indirect(offsets[:, q * PIECE_COLS : (q + 1) * PIECE_COLS])
-            nc.tensor.matmul(
-                banks[q][:], weights[:, a, :], picked,
-                start=(a == 0), stop=(a == K_BLOCKS - 1),
-            )
+        def gathered_matmul(a, i, begin, end, start, stop):
+            first = first_entry[i]
+            picked = windows[a][:].indirect(offsets[:, (first + begin) // 16 : (first + end) // 16])
+            nc.tensor.matmul(banks[i][:, begin:end], weights[:, a, :], picked, start=start, stop=stop)
 
-        for a in range(K_BLOCKS // 2):
-            for q in range(PIECES):
-                gathered_matmul(a, q)
+        def add_block(a, i):
+            for begin in range(0, BANK_ENTRIES[i], PIECE):
+                end = begin + PIECE
+                gathered_matmul(
+                    a, i, begin, end,
+                    start=False, stop=(a == K_BLOCKS - 1 and end == BANK_ENTRIES[i]),
+                )
+
+        for i in range(len(banks)):
+            gathered_matmul(0, i, 0, BANK_ENTRIES[i], start=True, stop=False)
+        for i in range(len(banks)):
+            add_block(1, i)
 
         pooled = held.tile([P, N // NEIGHBOURS], F32, name="pooled")
         result = held.tile([P, N // NEIGHBOURS], F32, name="result")
-        for q in range(PIECES):
-            for a in range(K_BLOCKS // 2, K_BLOCKS):
-                gathered_matmul(a, q)
-            nodes = slice(q * PIECE_NODES, (q + 1) * PIECE_NODES)
+        for i in range(len(banks)):
+            add_block(2, i)
+            add_block(3, i)
+            nodes = slice(first_entry[i] // NEIGHBOURS, (first_entry[i] + BANK_ENTRIES[i]) // NEIGHBOURS)
             nc.vector.tensor_reduce(
                 pooled[:, nodes],
-                banks[q][:].rearrange("p (v t) -> p v t", t=NEIGHBOURS),
+                banks[i][:].rearrange("p (v t) -> p v t", t=NEIGHBOURS),
                 axis=X, op=MAX,
             )
             nc.scalar.activation(result[:, nodes], pooled[:, nodes], TANH, bias=bias[:, 0:1])

@@ -21,10 +21,10 @@ def tile_gather_matmul_kernel(tc, table, w, b, offs, out):
         tc.tile_pool(name="held", bufs=1) as held,
         tc.psum_pool(name="psum", bufs=1) as psum,
     ):
-        offsets = held.tile([P, N // 16], U16, name="offsets")
-        nc.sync.dma_start(offsets[:], offs)
         weights = held.tile([P, K_BLOCKS, M], BF16, name="weights")
         nc.sync.dma_start(weights[:], w.rearrange("(p a) m -> p a m", a=K_BLOCKS))
+        offsets = held.tile([P, N // 16], U16, name="offsets")
+        nc.sync.dma_start(offsets[:], offs)
         table_blocks = table.rearrange("(p a) s -> a p s", a=K_BLOCKS)
         windows = [held.tile([P, S], BF16, name=f"window{a}") for a in range(K_BLOCKS)]
         for a in range(K_BLOCKS):

@@ -32,6 +32,11 @@ def tile_gather_matmul_kernel(tc, table, w, b, offs, out):
         bias = held.tile([P, 1], F32, name="bias")
         nc.sync.dma_start(bias[:], b)
 
+        zeros = held.tile([P, 1], F32, name="zeros")
+        nc.vector.memset(zeros[:], 0.0)
+        unused = held.tile([P, 1], F32, name="unused")
+        nc.scalar.activation(unused[:], zeros[:], TANH)
+
         banks = [
             psum.tile([P, entries], F32, name=f"bank{i}") for i, entries in enumerate(BANK_ENTRIES)
         ]

import concourse.mybir as mybir

BF16, F32, U16 = mybir.dt.bfloat16, mybir.dt.float32, mybir.dt.uint16
TANH = mybir.ActivationFunctionType.Tanh
MAX = mybir.AluOpType.max
X = mybir.AxisListType.X

P = 128
K, S, M, N = 512, 512, 128, 1024
NEIGHBOURS = 8
K_BLOCKS = K // P
PIECE = 256
BANK_ENTRIES = (2 * PIECE, PIECE, PIECE)

FLOPS = 2 * K * M * N


def tile_gather_matmul_kernel(tc, table, w, b, offs, out):
    nc = tc.nc
    with (
        tc.tile_pool(name="held", bufs=1) as held,
        tc.psum_pool(name="psum", bufs=1) as psum,
    ):
        weights = held.tile([P, K_BLOCKS, M], BF16, name="weights")
        nc.sync.dma_start(weights[:], w.rearrange("(p a) m -> p a m", a=K_BLOCKS))
        offsets = held.tile([P, N // 16], U16, name="offsets")
        nc.sync.dma_start(offsets[:], offs)
        table_blocks = table.rearrange("(p a) s -> a p s", a=K_BLOCKS)
        windows = [held.tile([P, S], BF16, name=f"window{a}") for a in range(K_BLOCKS)]
        for a in range(K_BLOCKS):
            nc.scalar.dma_start(windows[a][:], table_blocks[a])
        bias = held.tile([P, 1], F32, name="bias")
        nc.sync.dma_start(bias[:], b)

        zeros = held.tile([P, 1], F32, name="zeros")
        nc.vector.memset(zeros[:], 0.0)
        unused = held.tile([P, 1], F32, name="unused")
        nc.scalar.activation(unused[:], zeros[:], TANH)

        banks = [
            psum.tile([P, entries], F32, name=f"bank{i}") for i, entries in enumerate(BANK_ENTRIES)
        ]
        first_entry = [sum(BANK_ENTRIES[:i]) for i in range(len(BANK_ENTRIES))]

        def gathered_matmul(a, i, begin, end, start, stop):
            first = first_entry[i]
            picked = windows[a][:].indirect(offsets[:, (first + begin) // 16 : (first + end) // 16])
            nc.tensor.matmul(banks[i][:, begin:end], weights[:, a, :], picked, start=start, stop=stop)

        def add_block(a, i):
            for begin in range(0, BANK_ENTRIES[i], PIECE):
                end = begin + PIECE
                gathered_matmul(
                    a, i, begin, end,
                    start=False, stop=(a == K_BLOCKS - 1 and end == BANK_ENTRIES[i]),
                )

        for i in range(len(banks)):
            gathered_matmul(0, i, 0, BANK_ENTRIES[i], start=True, stop=False)
        for i in range(len(banks)):
            add_block(1, i)

        pooled = held.tile([P, N // NEIGHBOURS], F32, name="pooled")
        result = held.tile([P, N // NEIGHBOURS], F32, name="result")
        for i in range(len(banks)):
            add_block(2, i)
            add_block(3, i)
            nodes = slice(first_entry[i] // NEIGHBOURS, (first_entry[i] + BANK_ENTRIES[i]) // NEIGHBOURS)
            nc.vector.tensor_reduce(
                pooled[:, nodes],
                banks[i][:].rearrange("p (v t) -> p v t", t=NEIGHBOURS),
                axis=X, op=MAX,
            )
            nc.scalar.activation(result[:, nodes], pooled[:, nodes], TANH, bias=bias[:, 0:1])
        nc.sync.dma_start(out, result[:])
